import numpy as np
import ml_dtypes


def mxq(x, axis, fmt="e4m3"):
    dtype, down = {"e4m3": (ml_dtypes.float8_e4m3fn, 7), "e5m2": (ml_dtypes.float8_e5m2, 14)}[fmt]
    v = np.moveaxis(np.asarray(x, np.float32).astype(ml_dtypes.bfloat16).astype(np.float64), axis, -1)
    blocks = v.reshape(v.shape[:-1] + (-1, 32))
    amax = np.abs(blocks).max(-1, keepdims=True)
    byte = np.maximum(np.where(amax > 0, np.frexp(amax)[1] - 1 + 127, 0) - down, 1)
    scale = np.exp2(byte - 127.0)
    codes = (blocks / scale).astype(np.float32).astype(dtype).astype(np.float64)
    return np.moveaxis((codes * scale).reshape(v.shape), -1, axis)


WIDE = False


def mx_kscale(k):
    if not WIDE:
        return np.ones(k)
    levels = np.array([10, -10, 5, -5, 0])
    if k % 512:
        return np.exp2(np.random.permutation(np.resize(levels, k // 32))).repeat(32)
    a = np.empty((k // 512, 16))
    for p in range(k // 512):
        a[p, :8] = np.random.permutation(np.resize(levels, 8))
        for g in range(8):
            far = levels[np.abs(levels - a[p, g]) >= 10]
            a[p, g + 8] = far[np.random.randint(len(far))]
    return np.exp2(a.ravel()).repeat(32)


BF16 = ml_dtypes.bfloat16


def bf(x):
    return np.asarray(x, np.float32).astype(BF16)


def f64(x):
    return np.asarray(x).astype(np.float64)


T, D, F = 4096, 1024, 256


def erf(u):
    c = np.clip(u, -6.0, 6.0)
    q = 2.0 * c * c
    term = np.array(c)
    total = np.array(c)
    for n in range(1, 151):
        term *= q / (2 * n + 1)
        total += term
    return np.where(np.abs(u) > 6.0, np.sign(u), 2.0 / np.sqrt(np.pi) * np.exp(-c * c) * total)


def gelu_erf_grad(a):
    cdf = 0.5 * (1.0 + erf(a / np.sqrt(2.0)))
    pdf_term = a * np.exp(-np.square(a) / 2.0) / np.sqrt(2.0 * np.pi)
    return cdf + pdf_term


def frobenius(z):
    return np.sqrt(np.sum(np.square(z), axis=(0, 1)))


def draw0():
    s, t = mx_kscale(D), mx_kscale(T)
    return {
        "x": bf(np.random.standard_normal((T, D)) / t[:, None]),
        "a": bf(np.random.standard_normal((T, F))),
        "dy": bf(np.random.standard_normal((T, D)) * s[None, :] * t[:, None]),
        "w2": bf(np.random.standard_normal((F, D)) / np.sqrt(D) / s[None, :]),
        "w1": bf(np.random.standard_normal((D, F))),
        "m": bf(np.random.standard_normal((D, F)) * 0.3),
        "v": bf(np.random.uniform(0.2, 1.0, (D, F))),
    }


def core(x, a, dy, w2, w1, m, v):
    x, a, dy, w2, w1, m, v = f64(x), f64(a), f64(dy), f64(w2), f64(w1), f64(m), f64(v)
    tokens = x.shape[0]
    dh = mxq(dy, 1, "e4m3") @ mxq(w2, 1, "e4m3").T
    da = dh * gelu_erf_grad(a)
    g = (mxq(x, 0, "e4m3").T @ mxq(da, 0, "e4m3")) / np.sqrt(tokens)
    m_new = 0.6 * m + 0.4 * g
    v_new = 0.6 * v + 0.4 * np.square(g)
    r = m_new / np.sqrt(v_new) + 0.1 * w1
    trust = frobenius(w1) / frobenius(r)
    return w1 - 0.5 * trust * r


def e4m3fn_bytes(y):
    return np.clip(np.asarray(y, np.float64), -448.0, 448.0).astype(np.float32).astype(ml_dtypes.float8_e4m3fn).view(np.uint8)


def e4m3fn_values(b):
    return np.asarray(b, np.uint8).view(ml_dtypes.float8_e4m3fn).astype(np.float64)


def setup_inputs():
    d = draw0()
    x0 = np.asarray(d['x']).astype(np.float64)
    s = (np.max(np.abs(x0), axis=(1,), keepdims=True) / 448.0).astype(np.float32)
    out = {}
    for k, v in d.items():
        if k == 'x':
            out['x_bytes'] = e4m3fn_bytes(x0 / s.astype(np.float64))
            out['x_scale'] = s
        else:
            out[k] = v
    return out


def reference(x_bytes, x_scale, a, dy, w2, w1, m, v):
    return core(e4m3fn_values(x_bytes) * x_scale.astype(np.float64), a, dy, w2, w1, m, v)

@@ -1,0 +1,339 @@
+from contextlib import ExitStack
+
+import concourse.mybir as mybir
+from concourse.masks import make_identity
+
+F32 = mybir.dt.float32
+BF16 = mybir.dt.bfloat16
+U32 = mybir.dt.uint32
+U8 = mybir.dt.uint8
+FP8 = mybir.dt.float8_e4m3fn
+FP8X4 = mybir.dt.float8_e4m3fn_x4
+MULT = mybir.AluOpType.mult
+ADD = mybir.AluOpType.add
+MAX = mybir.AluOpType.max
+MIN = mybir.AluOpType.min
+ACT = mybir.ActivationFunctionType
+
+T, D, F = 4096, 1024, 256
+FLOPS = 4 * T * D * F
+
+P = 128
+NG = T // 512
+NC = D // 512
+NJ = D // P
+H = 1.5 * 2.0 ** -11
+
+
+def tile_lambmlpbackwardstep_t_kernel(tc, x_bytes, x_scale, a, dy, w2, w1, m, v, out):
+    nc = tc.nc
+    with ExitStack() as ctx:
+        keep = ctx.enter_context(tc.tile_pool(name="keep", bufs=1))
+        pool = ctx.enter_context(tc.tile_pool(name="work", bufs=2))
+        psum = ctx.enter_context(tc.psum_pool(name="psum", bufs=1))
+        ctx.enter_context(tc.manual_schedule())
+
+        ident = keep.tile([P, P], F32, name="ident")
+        ones = keep.tile([P, P], F32, name="ones")
+        offs = keep.tile([P, 4], F32, name="offs")
+        warm = keep.tile([P, 2], F32, name="warm")
+        xs = keep.tile([P, NG, 4], F32, name="xs")
+        xq = keep.tile([P, NG, D], U32, name="xq", align_bytes=64)
+        xqs = keep.tile([P, NG, D], U8, name="xqs", align_bytes=64)
+        daq = keep.tile([P, NG, F], U32, name="daq", align_bytes=64)
+        daqs = keep.tile([P, NG, F], U8, name="daqs", align_bytes=64)
+        w2r = keep.tile([P, 2, D], BF16, name="w2r", align_bytes=64)
+        w2g = keep.tile([P, NC * F * 4], BF16, name="w2g", align_bytes=64)
+        w2q = keep.tile([P, NC, F], U32, name="w2q", align_bytes=64)
+        w2qs = keep.tile([P, NC, F], U8, name="w2qs", align_bytes=64)
+        w1t = keep.tile([P, NJ, F], BF16, name="w1t")
+        mt = keep.tile([P, NJ, F], BF16, name="mt")
+        vt = keep.tile([P, NJ, F], BF16, name="vt")
+        sq = keep.tile([P, NJ, F], F32, name="sq")
+        mn = keep.tile([P, NJ, F], F32, name="mn")
+        stats = keep.tile([P, 8], F32, name="stats")
+        small = keep.tile([P, 8], F32, name="small")
+        wsum = keep.tile([P, 8], F32, name="wsum")
+        junk = keep.tile([P, 2, F], BF16, name="junk")
+
+        gbank = [psum.tile([P, 512], F32, name=f"g{j}", tag=f"g{j}", bufs=1) for j in range(4)]
+
+        a_v = a.rearrange("(g p t) f -> g p t f", p=P, t=4)
+        dy_v = dy.rearrange("(g p t) d -> g p t d", p=P, t=4)
+        x_v = x_bytes.rearrange("(g p t) d -> g p t d", p=P, t=4)
+
+        at, dyt, x8, ac, g3, g6, g2, dyg, dyq, dyqs, dh, da, xp, xi = ({} for k in range(14))
+
+        def load_a(i):
+            at[i] = pool.tile([P, 4 * F], BF16, name=f"a{i}", tag="a", bufs=3)
+            nc.sync.dma_start(out=at[i][:].rearrange("p (t f) -> p t f", t=4), in_=a_v[i])
+
+        def load_dy(i):
+            dyt[i] = pool.tile([P, 4, D], BF16, name=f"dy{i}", tag="dy", bufs=3)
+            nc.sync.dma_start(out=dyt[i][:], in_=dy_v[i])
+
+        def load_x(i):
+            x8[i] = pool.tile([P, 4, D], U8, name=f"x8_{i}", tag="x8", bufs=3)
+            nc.sync.dma_start(out=x8[i][:], in_=x_v[i])
+
+        def clamp(i):
+            ac[i] = pool.tile([P, 4 * F], BF16, name=f"ac{i}", tag="ac", bufs=2)
+            nc.vector.tensor_scalar(out=ac[i][:], in0=at[i][:], scalar1=7.0, scalar2=-7.0, op0=MIN, op1=MAX)
+
+        def gelu(i):
+            for d, tag, k in ((g6, "g6", 2), (g3, "g3", 1), (g2, "g2", 0)):
+                d[i] = pool.tile([P, 4 * F], F32, name=f"{tag}_{i}", tag=tag, bufs=2)
+                nc.scalar.activation(out=d[i][:], in_=ac[i][:], func=ACT.Gelu, bias=offs[:, k : k + 1])
+
+        def fd1(i):
+            nc.vector.scalar_tensor_tensor(out=g3[i][:], in0=g6[i][:], scalar=-5.0 / 32, in1=g3[i][:], op0=MULT, op1=ADD)
+
+        def fd2(i):
+            nc.vector.scalar_tensor_tensor(out=g2[i][:], in0=g2[i][:], scalar=-27.0 / 32, in1=g3[i][:], op0=MULT, op1=ADD)
+
+        def transposes(i, t):
+            bank = psum.tile([P, NC, 2, P], F32, name=f"tp{i}_{t}", tag="tp", bufs=2)
+            words = dyt[i][:, t, :].bitcast(F32)
+            for c in range(NC):
+                for u in range(2):
+                    nc.tensor.transpose(bank[:, c, u, :], words[:, 256 * c + u : 256 * (c + 1) : 2], ident[:])
+            if t == 0:
+                dyg[i] = pool.tile([P, 4, D], BF16, name=f"dyg{i}", tag="dyg", bufs=2, align_bytes=64)
+            dst = dyg[i][:, t, :].bitcast(F32).rearrange("q (c r u) -> q c r u", c=NC, u=2)
+            nc.scalar.copy(out=dst, in_=bank[:].rearrange("q c u r -> q c r u"))
+
+        def q_dy(i):
+            dyq[i] = pool.tile([P, 4, NC, P], U32, name=f"dyq{i}", tag="dyq", bufs=2, align_bytes=64)
+            dyqs[i] = pool.tile([P, 4, NC, P], U8, name=f"dyqs{i}", tag="dyqs", bufs=2, align_bytes=64)
+            for h in range(2):
+                s = slice(2 * h, 2 * h + 2)
+                nc.vector.quantize_mx(
+                    out=dyq[i][:, s].rearrange("p t c r -> p (t c r)").bitcast(FP8X4),
+                    scales=dyqs[i][:, s].rearrange("p t c r -> p (t c r)"),
+                    in_=dyg[i][:, s].rearrange("p t k -> p (t k)"),
+                )
+
+        def mm1(i):
+            for h in range(2):
+                dh[i, h] = psum.tile([P, 4, P], F32, name=f"dh{i}_{h}", tag="dh", bufs=2)
+                for t in range(4):
+                    for c in range(NC):
+                        nc.tensor.matmul_mx(
+                            out=dh[i, h][:, t, :],
+                            lhsT=dyq[i][:, t, c, :].bitcast(FP8X4),
+                            lhsT_scale=dyqs[i][:, t, c, :],
+                            rhs=w2q[:, c, 128 * h : 128 * (h + 1)].bitcast(FP8X4),
+                            rhs_scale=w2qs[:, c, 128 * h : 128 * (h + 1)],
+                            start=(c == 0),
+                            stop=(c == NC - 1),
+                        )
+
+        def make_da(i):
+            da[i] = pool.tile([P, F, 4], BF16, name=f"da{i}", tag="da", bufs=2, align_bytes=64)
+            wv = g2[i][:].rearrange("p (t f) -> p f t", t=4)
+            for h in range(2):
+                nc.vector.scalar_tensor_tensor(
+                    out=da[i][:, 128 * h : 128 * (h + 1), :],
+                    in0=wv[:, 128 * h : 128 * (h + 1), :],
+                    scalar=4.0 / (15.0 * H),
+                    in1=dh[i, h][:].rearrange("p t f -> p f t"),
+                    op0=MULT,
+                    op1=MULT,
+                )
+
+        def q_da(i):
+            nc.vector.quantize_mx(
+                out=daq[:, i, :].bitcast(FP8X4), scales=daqs[:, i, :], in_=da[i][:].rearrange("p f t -> p (f t)")
+            )
+
+        def widen(i, t):
+            if t == 0:
+                xp[i] = pool.tile([P, 2, D, 2], BF16, name=f"xp{i}", tag="xp", bufs=2)
+            nc.vector.tensor_scalar(
+                out=xp[i][:, t // 2, :, t % 2], in0=x8[i][:, t, :].bitcast(FP8), scalar1=xs[:, i, t : t + 1], scalar2=None, op0=MULT
+            )
+
+        def pair_up(i, h):
+            if h == 0:
+                xi[i] = pool.tile([P, D * 4], BF16, name=f"xi{i}", tag="xi", bufs=2, align_bytes=64)
+            src = xp[i][:].rearrange("p a d e -> p (a d e)").bitcast(F32).rearrange("p (a d) -> p d a", a=2)
+            dst = xi[i][:].bitcast(F32).rearrange("p (d a) -> p d a", a=2)
+            s = slice(512 * h, 512 * (h + 1))
+            nc.scalar.copy(out=dst[:, s, :], in_=src[:, s, :])
+
+        def q_x(i, h):
+            s = slice(512 * h, 512 * (h + 1))
+            nc.vector.quantize_mx(
+                out=xq[:, i, s].bitcast(FP8X4), scales=xqs[:, i, s], in_=xi[i][:, 2048 * h : 2048 * (h + 1)]
+            )
+
+        def mm2(i, js):
+            for j in js:
+                nc.tensor.matmul_mx(
+                    out=gbank[j][:, 0:F],
+                    lhsT=xq[:, i, P * j : P * (j + 1)].bitcast(FP8X4),
+                    lhsT_scale=xqs[:, i, P * j : P * (j + 1)],
+                    rhs=daq[:, i, :].bitcast(FP8X4),
+                    rhs_scale=daqs[:, i, :],
+                    start=(i == 0),
+                    stop=(i == NG - 1),
+                )
+
+        load_a(0)
+        nc.scalar.dma_start(out=xs[:], in_=x_scale.rearrange("(g p t) o -> p g (t o)", p=P, t=4))
+        load_x(0)
+        load_dy(0)
+        nc.sync.dma_start(out=w2r[:], in_=w2.rearrange("(h p) d -> p h d", p=P))
+        load_a(1)
+        load_x(1)
+        load_dy(1)
+        nc.vector.memset(warm[:], 1.0)
+        for k, n in enumerate((-2.0, 3.0, 6.0)):
+            nc.vector.memset(offs[:, k : k + 1], n * H)
+        nc.vector.memset(ones[:], 1.0)
+        nc.scalar.activation(out=warm[:, 0:1], in_=warm[:, 1:2], func=ACT.Gelu, bias=offs[:, 0:1])
+        make_identity(nc, ident[:])
+        clamp(0)
+
+        def prep_w2():
+            dst = w2g[:].bitcast(F32).rearrange("q (c f u) -> q c f u", c=NC, u=2)
+            for h in range(2):
+                bank = psum.tile([P, NC, 2, P], F32, name=f"tpw{h}", tag="tp", bufs=2)
+                words = w2r[:, h, :].bitcast(F32)
+                for c in range(NC):
+                    for u in range(2):
+                        nc.tensor.transpose(bank[:, c, u, :], words[:, 256 * c + u : 256 * (c + 1) : 2], ident[:])
+                nc.vector.tensor_copy(out=dst[:, :, P * h : P * (h + 1), :], in_=bank[:].rearrange("q c u r -> q c r u"))
+            nc.vector.quantize_mx(
+                out=w2q[:].rearrange("p c f -> p (c f)").bitcast(FP8X4), scales=w2qs[:].rearrange("p c f -> p (c f)"), in_=w2g[:]
+            )
+
+        def w1_norm(b):
+            s = slice(2 * b, 2 * b + 2)
+            nc.scalar.activation(out=junk[:], in_=w1t[:, s, :], func=ACT.Square, accum_out=stats[:, b : b + 1])
+
+        for s in range(NG + 1):
+            if s + 2 < NG:
+                load_a(s + 2)
+                load_x(s + 2)
+                load_dy(s + 2)
+            if s == 2:
+                nc.sync.dma_start(out=w1t[:], in_=w1.rearrange("(j p) f -> p j f", p=P))
+            if s == 4:
+                nc.sync.dma_start(out=mt[:], in_=m.rearrange("(j p) f -> p j f", p=P))
+                nc.sync.dma_start(out=vt[:], in_=v.rearrange("(j p) f -> p j f", p=P))
+            if s >= 1:
+                q_dy(s - 1)
+                mm1(s - 1)
+            if s < NG:
+                gelu(s)
+                widen(s, 0)
+                widen(s, 1)
+                widen(s, 2)
+                widen(s, 3)
+                transposes(s, 0)
+                transposes(s, 1)
+                if s + 1 < NG:
+                    clamp(s + 1)
+                fd1(s)
+                if s >= 1:
+                    q_x(s - 1, 0)
+                    q_x(s - 1, 1)
+                fd2(s)
+                if s >= 2:
+                    mm2(s - 2, range(4))
+                if s == NG - 1:
+                    wtot = psum.tile([P, 8], F32, name="wtot", tag="tp", bufs=2)
+                    for b in range(4):
+                        nc.tensor.matmul(wtot[:, 0:1], lhsT=ones[:], rhs=stats[:, b : b + 1], start=(b == 0), stop=(b == 3))
+                    nc.vector.tensor_copy(out=wsum[:, 0:1], in_=wtot[:, 0:1])
+                transposes(s, 2)
+                transposes(s, 3)
+                if s == 0:
+                    prep_w2()
+                if s >= 1:
+                    make_da(s - 1)
+                pair_up(s, 0)
+                if 3 <= s < 7:
+                    w1_norm(s - 3)
+                pair_up(s, 1)
+                if s >= 1:
+                    q_da(s - 1)
+        nc.scalar.activation(out=warm[:, 0:1], in_=warm[:, 1:2], func=ACT.Abs_reciprocal_sqrt)
+        q_x(NG - 1, 0)
+        mm2(NG - 2, range(4))
+        gbank.append(psum.tile([P, 512], F32, name="g4", tag="tp", bufs=2))
+        for i in range(NG - 1):
+            mm2(i, [4])
+        make_da(NG - 1)
+        q_da(NG - 1)
+        q_x(NG - 1, 1)
+        mm2(NG - 1, range(4))
+        mm2(NG - 1, [4])
+        for j, tag in ((5, "dh"), (6, "dh"), (7, "tp")):
+            gbank.append(psum.tile([P, 512], F32, name=f"g{j}", tag=tag, bufs=2))
+            for i in range(NG):
+                mm2(i, [j])
+
+        def moments(b):
+            for js, jv in ((2 * b, 2 * b + 1), (2 * b + 1, 2 * b)):
+                nc.scalar.activation(
+                    out=sq[:, js, :], in_=gbank[js][:, 0:F], func=ACT.Square, scale=(2.0 / 3.0) ** 0.5 / 64.0
+                )
+                nc.vector.scalar_tensor_tensor(
+                    out=mn[:, jv, :], in0=gbank[jv][:, 0:F], scalar=2.0 / 3.0 / 64.0, in1=mt[:, jv, :], op0=MULT, op1=ADD
+                )
+            s = slice(2 * b, 2 * b + 2)
+            nc.gpsimd.tensor_tensor(out=sq[:, s, :], in0=sq[:, s, :], in1=vt[:, s, :], op=ADD)
+
+        def inv_root(b):
+            s = slice(2 * b, 2 * b + 2)
+            nc.scalar.activation(out=sq[:, s, :], in_=sq[:, s, :], func=ACT.Abs_reciprocal_sqrt, scale=1.0 / 0.6)
+
+        def ratio(b):
+            s = slice(2 * b, 2 * b + 2)
+            nc.vector.tensor_tensor(out=mn[:, s, :], in0=mn[:, s, :], in1=sq[:, s, :], op=MULT)
+
+        def decay(b):
+            s = slice(2 * b, 2 * b + 2)
+            nc.vector.scalar_tensor_tensor(out=mn[:, s, :], in0=w1t[:, s, :], scalar=0.1, in1=mn[:, s, :], op0=MULT, op1=ADD)
+
+        def r_norm(b):
+            s = slice(2 * b, 2 * b + 2)
+            nc.scalar.activation(out=sq[:, s, :], in_=mn[:, s, :], func=ACT.Square, accum_out=stats[:, 4 + b : 5 + b])
+
+        moments(0)
+        moments(1)
+        inv_root(0)
+        moments(2)
+        ratio(0)
+        inv_root(1)
+        moments(3)
+        decay(0)
+        ratio(1)
+        inv_root(2)
+        r_norm(0)
+        decay(1)
+        ratio(2)
+        inv_root(3)
+        r_norm(1)
+        decay(2)
+        ratio(3)
+        r_norm(2)
+        decay(3)
+        r_norm(3)
+        tot = psum.tile([P, 8], F32, name="rtot", tag="tp", bufs=2)
+        for b in range(4):
+            nc.tensor.matmul(tot[:, 0:1], lhsT=ones[:], rhs=stats[:, 4 + b : 5 + b], start=(b == 0), stop=(b == 3))
+        nc.scalar.activation(out=small[:, 0:1], in_=tot[:, 0:1], func=ACT.Abs_reciprocal_sqrt, scale=wsum[:, 0:1])
+        nc.vector.tensor_scalar(
+            out=small[:, 4:5], in0=small[:, 0:1], scalar1=wsum[:, 0:1], scalar2=-0.5, op0=MULT, op1=MULT
+        )
+        out_v = out.rearrange("(j p) f -> p j f", p=P)
+        for b in range(4):
+            s = slice(2 * b, 2 * b + 2)
+            res = pool.tile([P, 2, F], F32, name=f"res{b}", tag="res", bufs=4)
+            nc.vector.scalar_tensor_tensor(
+                out=res[:], in0=mn[:, s, :], scalar=small[:, 4:5], in1=w1t[:, s, :], op0=MULT, op1=ADD
+            )
+            nc.sync.dma_start(out=out_v[:, s, :], in_=res[:])

@@ -11,6 +11,7 @@ FP8 = mybir.dt.float8_e4m3fn
 FP8X4 = mybir.dt.float8_e4m3fn_x4
 MULT = mybir.AluOpType.mult
 ADD = mybir.AluOpType.add
+SUB = mybir.AluOpType.subtract
 MAX = mybir.AluOpType.max
 MIN = mybir.AluOpType.min
 ACT = mybir.ActivationFunctionType
@@ -23,6 +24,15 @@ NG = T // 512
 NC = D // 512
 NJ = D // P
 H = 1.5 * 2.0 ** -11
+LIVE = 3
+
+
+def on_tensor(i, h):
+    return h == 0 or i in (1,3,5,6)
+
+
+def by_plane(i):
+    return i in (1,3,5)
 
 
 def tile_lambmlpbackwardstep_t_kernel(tc, x_bytes, x_scale, a, dy, w2, w1, m, v, out):
@@ -35,6 +45,7 @@ def tile_lambmlpbackwardstep_t_kernel(tc, x_bytes, x_scale, a, dy, w2, w1, m, v,
 
         ident = keep.tile([P, P], F32, name="ident")
         ones = keep.tile([P, P], F32, name="ones")
+        ident_b = keep.tile([P, P], F32, name="ident_b")
         offs = keep.tile([P, 4], F32, name="offs")
         warm = keep.tile([P, 2], F32, name="warm")
         xs = keep.tile([P, NG, 4], F32, name="xs")
@@ -56,13 +67,13 @@ def tile_lambmlpbackwardstep_t_kernel(tc, x_bytes, x_scale, a, dy, w2, w1, m, v,
         wsum = keep.tile([P, 8], F32, name="wsum")
         junk = keep.tile([P, 2, F], BF16, name="junk")
 
-        gbank = [psum.tile([P, 512], F32, name=f"g{j}", tag=f"g{j}", bufs=1) for j in range(4)]
+        gbank = [psum.tile([P, 512], F32, name=f"g{j}", tag=f"g{j}", bufs=1) for j in range(LIVE)]
 
         a_v = a.rearrange("(g p t) f -> g p t f", p=P, t=4)
         dy_v = dy.rearrange("(g p t) d -> g p t d", p=P, t=4)
         x_v = x_bytes.rearrange("(g p t) d -> g p t d", p=P, t=4)
 
-        at, dyt, x8, ac, g3, g6, g2, dyg, dyq, dyqs, dh, da, xp, xi = ({} for k in range(14))
+        at, dyt, x8, ac, g3, g6, g2, dyg, dyq, dyqs, dh, da, xp, xi, fd, tp = ({} for k in range(16))
 
         def load_a(i):
             at[i] = pool.tile([P, 4 * F], BF16, name=f"a{i}", tag="a", bufs=3)
@@ -80,27 +91,41 @@ def tile_lambmlpbackwardstep_t_kernel(tc, x_bytes, x_scale, a, dy, w2, w1, m, v,
             ac[i] = pool.tile([P, 4 * F], BF16, name=f"ac{i}", tag="ac", bufs=2)
             nc.vector.tensor_scalar(out=ac[i][:], in0=at[i][:], scalar1=7.0, scalar2=-7.0, op0=MIN, op1=MAX)
 
-        def gelu(i):
-            for d, tag, k in ((g6, "g6", 2), (g3, "g3", 1), (g2, "g2", 0)):
+        def gelu(i, nodes):
+            for n in nodes:
+                d, tag, k = ((g2, "g2", 0), (g3, "g3", 1), (g6, "g6", 2))[n]
                 d[i] = pool.tile([P, 4 * F], F32, name=f"{tag}_{i}", tag=tag, bufs=2)
                 nc.scalar.activation(out=d[i][:], in_=ac[i][:], func=ACT.Gelu, bias=offs[:, k : k + 1])
 
-        def fd1(i):
-            nc.vector.scalar_tensor_tensor(out=g3[i][:], in0=g6[i][:], scalar=-5.0 / 32, in1=g3[i][:], op0=MULT, op1=ADD)
+        def fd_mm(i, h):
+            s = slice(512 * h, 512 * (h + 1))
+            if on_tensor(i, h):
+                fd[i, h] = psum.tile([P, 512], F32, name=f"fd{i}_{h}", tag="fd", bufs=1)
+                nc.tensor.matmul(fd[i, h][:], lhsT=ident_b[:], rhs=g2[i][:, s], start=True, stop=False)
+                nc.tensor.matmul(fd[i, h][:], lhsT=ident[:], rhs=g3[i][:, s], start=False, stop=True)
 
-        def fd2(i):
-            nc.vector.scalar_tensor_tensor(out=g2[i][:], in0=g2[i][:], scalar=-27.0 / 32, in1=g3[i][:], op0=MULT, op1=ADD)
+        def fd1(i, h):
+            s = slice(512 * h, 512 * (h + 1))
+            if not on_tensor(i, h):
+                nc.vector.scalar_tensor_tensor(out=g3[i][:, s], in0=g2[i][:, s], scalar=-27.0 / 32, in1=g3[i][:, s], op0=MULT, op1=ADD)
 
-        def transposes(i, t):
-            bank = psum.tile([P, NC, 2, P], F32, name=f"tp{i}_{t}", tag="tp", bufs=2)
+        def fd2(i, h):
+            s = slice(512 * h, 512 * (h + 1))
+            part = fd[i, h][:] if on_tensor(i, h) else g3[i][:, s]
+            nc.vector.scalar_tensor_tensor(out=g6[i][:, s], in0=g6[i][:, s], scalar=-5.0 / 32, in1=part, op0=MULT, op1=ADD)
+
+        def transposes_pe(i, t):
+            tp[i, t] = psum.tile([P, NC, 2, P], F32, name=f"tp{i}_{t}", tag="tp", bufs=2)
             words = dyt[i][:, t, :].bitcast(F32)
             for c in range(NC):
                 for u in range(2):
-                    nc.tensor.transpose(bank[:, c, u, :], words[:, 256 * c + u : 256 * (c + 1) : 2], ident[:])
+                    nc.tensor.transpose(tp[i, t][:, c, u, :], words[:, 256 * c + u : 256 * (c + 1) : 2], ident[:])
+
+        def copy_t(i, t):
             if t == 0:
                 dyg[i] = pool.tile([P, 4, D], BF16, name=f"dyg{i}", tag="dyg", bufs=2, align_bytes=64)
             dst = dyg[i][:, t, :].bitcast(F32).rearrange("q (c r u) -> q c r u", c=NC, u=2)
-            nc.scalar.copy(out=dst, in_=bank[:].rearrange("q c u r -> q c r u"))
+            nc.scalar.copy(out=dst, in_=tp[i, t][:].rearrange("q c u r -> q c r u"))
 
         def q_dy(i):
             dyq[i] = pool.tile([P, 4, NC, P], U32, name=f"dyq{i}", tag="dyq", bufs=2, align_bytes=64)
@@ -130,7 +155,7 @@ def tile_lambmlpbackwardstep_t_kernel(tc, x_bytes, x_scale, a, dy, w2, w1, m, v,
 
         def make_da(i):
             da[i] = pool.tile([P, F, 4], BF16, name=f"da{i}", tag="da", bufs=2, align_bytes=64)
-            wv = g2[i][:].rearrange("p (t f) -> p f t", t=4)
+            wv = g6[i][:].rearrange("p (t f) -> p f t", t=4)
             for h in range(2):
                 nc.vector.scalar_tensor_tensor(
                     out=da[i][:, 128 * h : 128 * (h + 1), :],
@@ -148,17 +173,23 @@ def tile_lambmlpbackwardstep_t_kernel(tc, x_bytes, x_scale, a, dy, w2, w1, m, v,
 
         def widen(i, t):
             if t == 0:
-                xp[i] = pool.tile([P, 2, D, 2], BF16, name=f"xp{i}", tag="xp", bufs=2)
-            nc.vector.tensor_scalar(
-                out=xp[i][:, t // 2, :, t % 2], in0=x8[i][:, t, :].bitcast(FP8), scalar1=xs[:, i, t : t + 1], scalar2=None, op0=MULT
-            )
+                xp[i] = pool.tile([P, 4 * D], BF16, name=f"xp{i}", tag="xp", bufs=2)
+            if by_plane(i):
+                dst = xp[i][:, D * t : D * (t + 1)]
+            else:
+                dst = xp[i][:].rearrange("p (a d e) -> p a d e", a=2, e=2)[:, t // 2, :, t % 2]
+            nc.vector.tensor_scalar(out=dst, in0=x8[i][:, t, :].bitcast(FP8), scalar1=xs[:, i, t : t + 1], scalar2=None, op0=MULT)
 
         def pair_up(i, h):
             if h == 0:
                 xi[i] = pool.tile([P, D * 4], BF16, name=f"xi{i}", tag="xi", bufs=2, align_bytes=64)
-            src = xp[i][:].rearrange("p a d e -> p (a d e)").bitcast(F32).rearrange("p (a d) -> p d a", a=2)
-            dst = xi[i][:].bitcast(F32).rearrange("p (d a) -> p d a", a=2)
             s = slice(512 * h, 512 * (h + 1))
+            if by_plane(i):
+                src = xp[i][:].rearrange("p (t d) -> p d t", t=4)
+                dst = xi[i][:].rearrange("p (d t) -> p d t", t=4)
+            else:
+                src = xp[i][:].bitcast(F32).rearrange("p (a d) -> p d a", a=2)
+                dst = xi[i][:].bitcast(F32).rearrange("p (d a) -> p d a", a=2)
             nc.scalar.copy(out=dst[:, s, :], in_=src[:, s, :])
 
         def q_x(i, h):
@@ -182,8 +213,8 @@ def tile_lambmlpbackwardstep_t_kernel(tc, x_bytes, x_scale, a, dy, w2, w1, m, v,
         load_a(0)
         nc.scalar.dma_start(out=xs[:], in_=x_scale.rearrange("(g p t) o -> p g (t o)", p=P, t=4))
         load_x(0)
-        load_dy(0)
         nc.sync.dma_start(out=w2r[:], in_=w2.rearrange("(h p) d -> p h d", p=P))
+        load_dy(0)
         load_a(1)
         load_x(1)
         load_dy(1)
@@ -193,24 +224,28 @@ def tile_lambmlpbackwardstep_t_kernel(tc, x_bytes, x_scale, a, dy, w2, w1, m, v,
         nc.vector.memset(ones[:], 1.0)
         nc.scalar.activation(out=warm[:, 0:1], in_=warm[:, 1:2], func=ACT.Gelu, bias=offs[:, 0:1])
         make_identity(nc, ident[:])
+        nc.vector.tensor_scalar(out=ident_b[:], in0=ident[:], scalar1=-27.0 / 32, scalar2=None, op0=MULT)
         clamp(0)
 
-        def prep_w2():
+        def w2_transposes(h):
+            bank = psum.tile([P, NC, 2, P], F32, name=f"w2_{h}", tag="dh", bufs=2)
+            words = w2r[:, h, :].bitcast(F32)
+            for c in range(NC):
+                for u in range(2):
+                    nc.tensor.transpose(bank[:, c, u, :], words[:, 256 * c + u : 256 * (c + 1) : 2], ident[:])
+            return bank
+
+        def prep_w2(banks):
             dst = w2g[:].bitcast(F32).rearrange("q (c f u) -> q c f u", c=NC, u=2)
             for h in range(2):
-                bank = psum.tile([P, NC, 2, P], F32, name=f"tpw{h}", tag="tp", bufs=2)
-                words = w2r[:, h, :].bitcast(F32)
-                for c in range(NC):
-                    for u in range(2):
-                        nc.tensor.transpose(bank[:, c, u, :], words[:, 256 * c + u : 256 * (c + 1) : 2], ident[:])
-                nc.vector.tensor_copy(out=dst[:, :, P * h : P * (h + 1), :], in_=bank[:].rearrange("q c u r -> q c r u"))
+                nc.vector.tensor_copy(out=dst[:, :, P * h : P * (h + 1), :], in_=banks[h][:].rearrange("q c u r -> q c r u"))
             nc.vector.quantize_mx(
                 out=w2q[:].rearrange("p c f -> p (c f)").bitcast(FP8X4), scales=w2qs[:].rearrange("p c f -> p (c f)"), in_=w2g[:]
             )
 
         def w1_norm(b):
             s = slice(2 * b, 2 * b + 2)
-            nc.scalar.activation(out=junk[:], in_=w1t[:, s, :], func=ACT.Square, accum_out=stats[:, b : b + 1])
+            nc.scalar.activation(out=junk[:], in_=w1t[:, s, :], func=ACT.Square, scale=0.5, accum_out=stats[:, b : b + 1])
 
         for s in range(NG + 1):
             if s + 2 < NG:
@@ -222,66 +257,96 @@ def tile_lambmlpbackwardstep_t_kernel(tc, x_bytes, x_scale, a, dy, w2, w1, m, v,
             if s == 4:
                 nc.sync.dma_start(out=mt[:], in_=m.rearrange("(j p) f -> p j f", p=P))
                 nc.sync.dma_start(out=vt[:], in_=v.rearrange("(j p) f -> p j f", p=P))
-            if s >= 1:
-                q_dy(s - 1)
-                mm1(s - 1)
+            if s == 0:
+                w2_banks = [w2_transposes(h) for h in range(2)]
+            if s == 0:
+                gelu(0, range(3))
             if s < NG:
-                gelu(s)
                 widen(s, 0)
-                widen(s, 1)
-                widen(s, 2)
+            if s < NG:
+                transposes_pe(s, 0)
+            if 1 <= s:
+                fd1(s - 1, 0)
+            if s < NG:
+                transposes_pe(s, 1)
+            if s < NG:
                 widen(s, 3)
-                transposes(s, 0)
-                transposes(s, 1)
-                if s + 1 < NG:
-                    clamp(s + 1)
-                fd1(s)
-                if s >= 1:
-                    q_x(s - 1, 0)
-                    q_x(s - 1, 1)
-                fd2(s)
-                if s >= 2:
-                    mm2(s - 2, range(4))
-                if s == NG - 1:
-                    wtot = psum.tile([P, 8], F32, name="wtot", tag="tp", bufs=2)
-                    for b in range(4):
-                        nc.tensor.matmul(wtot[:, 0:1], lhsT=ones[:], rhs=stats[:, b : b + 1], start=(b == 0), stop=(b == 3))
-                    nc.vector.tensor_copy(out=wsum[:, 0:1], in_=wtot[:, 0:1])
-                transposes(s, 2)
-                transposes(s, 3)
-                if s == 0:
-                    prep_w2()
-                if s >= 1:
-                    make_da(s - 1)
+            if 1 <= s:
+                q_dy(s - 1)
+            if 1 <= s:
+                fd1(s - 1, 1)
+            if 0 < s < NG:
+                gelu(s, [0])
+            if 2 <= s and s - 2 < NG - 1:
+                q_da(s - 2)
+            if 1 <= s:
+                fd2(s - 1, 0)
+            if 1 <= s:
+                fd_mm(s - 1, 1)
+            if 1 <= s:
+                mm1(s - 1)
+            if 1 <= s:
+                q_x(s - 1, 0)
+            if s < NG:
+                copy_t(s, 0)
+            if s < NG:
+                transposes_pe(s, 2)
+            if s < NG:
+                widen(s, 1)
+            if s == 0:
+                prep_w2(w2_banks)
+            if s < NG:
+                widen(s, 2)
+            if s < NG:
+                copy_t(s, 1)
+            if s < NG:
+                transposes_pe(s, 3)
+            if s + 1 < NG:
+                clamp(s + 1)
+            if 1 <= s:
+                fd2(s - 1, 1)
+            if 0 < s < NG:
+                gelu(s, [1])
+            if s < NG:
+                copy_t(s, 2)
+            if s < NG:
+                copy_t(s, 3)
+            if 1 <= s:
+                q_x(s - 1, 1)
+            if 0 < s < NG:
+                gelu(s, [2])
+            if s < NG:
                 pair_up(s, 0)
-                if 3 <= s < 7:
-                    w1_norm(s - 3)
+            if s < NG:
+                fd_mm(s, 0)
+            if 2 <= s and s - 2 < NG - 1:
+                mm2(s - 2, range(LIVE))
+            if s < NG:
                 pair_up(s, 1)
-                if s >= 1:
-                    q_da(s - 1)
-        nc.scalar.activation(out=warm[:, 0:1], in_=warm[:, 1:2], func=ACT.Abs_reciprocal_sqrt)
-        q_x(NG - 1, 0)
-        mm2(NG - 2, range(4))
-        gbank.append(psum.tile([P, 512], F32, name="g4", tag="tp", bufs=2))
-        for i in range(NG - 1):
-            mm2(i, [4])
-        make_da(NG - 1)
+            if 1 <= s:
+                make_da(s - 1)
+            if s == NG - 1:
+                for b in range(4):
+                    w1_norm(b)
+                nc.scalar.activation(out=warm[:, 0:1], in_=warm[:, 1:2], func=ACT.Abs_reciprocal_sqrt)
+            if s == NG:
+                for j, tag in ((3, "fd"), (4, "tp"), (5, "tp")):
+                    gbank.append(psum.tile([P, 512], F32, name=f"g{j}", tag=tag, bufs=1 if tag == "fd" else 2))
+                    for i in range(NG - 1):
+                        mm2(i, [j])
         q_da(NG - 1)
-        q_x(NG - 1, 1)
-        mm2(NG - 1, range(4))
-        mm2(NG - 1, [4])
-        for j, tag in ((5, "dh"), (6, "dh"), (7, "tp")):
-            gbank.append(psum.tile([P, 512], F32, name=f"g{j}", tag=tag, bufs=2))
+        mm2(NG - 1, range(6))
+        for j in (6, 7):
+            gbank.append(psum.tile([P, 512], F32, name=f"g{j}", tag="dh", bufs=2))
             for i in range(NG):
                 mm2(i, [j])
-
         def moments(b):
             for js, jv in ((2 * b, 2 * b + 1), (2 * b + 1, 2 * b)):
                 nc.scalar.activation(
                     out=sq[:, js, :], in_=gbank[js][:, 0:F], func=ACT.Square, scale=(2.0 / 3.0) ** 0.5 / 64.0
                 )
                 nc.vector.scalar_tensor_tensor(
-                    out=mn[:, jv, :], in0=gbank[jv][:, 0:F], scalar=2.0 / 3.0 / 64.0, in1=mt[:, jv, :], op0=MULT, op1=ADD
+                    out=mn[:, jv, :], in0=gbank[jv][:, 0:F], scalar=-2.0 / 3.0 / 64.0, in1=mt[:, jv, :], op0=MULT, op1=SUB
                 )
             s = slice(2 * b, 2 * b + 2)
             nc.gpsimd.tensor_tensor(out=sq[:, s, :], in0=sq[:, s, :], in1=vt[:, s, :], op=ADD)
@@ -296,7 +361,7 @@ def tile_lambmlpbackwardstep_t_kernel(tc, x_bytes, x_scale, a, dy, w2, w1, m, v,
 
         def decay(b):
             s = slice(2 * b, 2 * b + 2)
-            nc.vector.scalar_tensor_tensor(out=mn[:, s, :], in0=w1t[:, s, :], scalar=0.1, in1=mn[:, s, :], op0=MULT, op1=ADD)
+            nc.vector.scalar_tensor_tensor(out=mn[:, s, :], in0=w1t[:, s, :], scalar=-0.1, in1=mn[:, s, :], op0=MULT, op1=ADD)
 
         def r_norm(b):
             s = slice(2 * b, 2 * b + 2)
@@ -304,36 +369,36 @@ def tile_lambmlpbackwardstep_t_kernel(tc, x_bytes, x_scale, a, dy, w2, w1, m, v,
 
         moments(0)
         moments(1)
-        inv_root(0)
         moments(2)
-        ratio(0)
-        inv_root(1)
+        inv_root(0)
         moments(3)
-        decay(0)
-        ratio(1)
+        inv_root(1)
+        ratio(0)
         inv_root(2)
+        ratio(1)
+        decay(0)
         r_norm(0)
-        decay(1)
-        ratio(2)
         inv_root(3)
+        ratio(2)
+        decay(1)
         r_norm(1)
-        decay(2)
         ratio(3)
+        decay(2)
         r_norm(2)
+        tot = psum.tile([P, 8], F32, name="tot", tag="g0", bufs=1)
+        for b in range(4):
+            nc.tensor.matmul(tot[:, 1:2], lhsT=ones[:], rhs=stats[:, b : b + 1], start=(b == 0), stop=(b == 3))
         decay(3)
+        nc.vector.reciprocal(out=wsum[:, 0:1], in_=tot[:, 1:2])
         r_norm(3)
-        tot = psum.tile([P, 8], F32, name="rtot", tag="tp", bufs=2)
         for b in range(4):
             nc.tensor.matmul(tot[:, 0:1], lhsT=ones[:], rhs=stats[:, 4 + b : 5 + b], start=(b == 0), stop=(b == 3))
         nc.scalar.activation(out=small[:, 0:1], in_=tot[:, 0:1], func=ACT.Abs_reciprocal_sqrt, scale=wsum[:, 0:1])
-        nc.vector.tensor_scalar(
-            out=small[:, 4:5], in0=small[:, 0:1], scalar1=wsum[:, 0:1], scalar2=-0.5, op0=MULT, op1=MULT
-        )
         out_v = out.rearrange("(j p) f -> p j f", p=P)
         for b in range(4):
             s = slice(2 * b, 2 * b + 2)
             res = pool.tile([P, 2, F], F32, name=f"res{b}", tag="res", bufs=4)
             nc.vector.scalar_tensor_tensor(
-                out=res[:], in0=mn[:, s, :], scalar=small[:, 4:5], in1=w1t[:, s, :], op0=MULT, op1=ADD
+                out=res[:], in0=mn[:, s, :], scalar=small[:, 0:1], in1=w1t[:, s, :], op0=MULT, op1=ADD
             )
             nc.sync.dma_start(out=out_v[:, s, :], in_=res[:])

@@ -24,15 +24,11 @@ NG = T // 512
 NC = D // 512
 NJ = D // P
 H = 1.5 * 2.0 ** -11
-LIVE = 3
-
-
-def on_tensor(i, h):
-    return h == 0 or i in (1,3,5,6)
+LIVE = 4
 
 
 def by_plane(i):
-    return i in (1,3,5)
+    return i in (1,3,5,7)
 
 
 def tile_lambmlpbackwardstep_t_kernel(tc, x_bytes, x_scale, a, dy, w2, w1, m, v, out):
@@ -45,7 +41,6 @@ def tile_lambmlpbackwardstep_t_kernel(tc, x_bytes, x_scale, a, dy, w2, w1, m, v,
 
         ident = keep.tile([P, P], F32, name="ident")
         ones = keep.tile([P, P], F32, name="ones")
-        ident_b = keep.tile([P, P], F32, name="ident_b")
         offs = keep.tile([P, 4], F32, name="offs")
         warm = keep.tile([P, 2], F32, name="warm")
         xs = keep.tile([P, NG, 4], F32, name="xs")
@@ -73,7 +68,7 @@ def tile_lambmlpbackwardstep_t_kernel(tc, x_bytes, x_scale, a, dy, w2, w1, m, v,
         dy_v = dy.rearrange("(g p t) d -> g p t d", p=P, t=4)
         x_v = x_bytes.rearrange("(g p t) d -> g p t d", p=P, t=4)
 
-        at, dyt, x8, ac, g3, g6, g2, dyg, dyq, dyqs, dh, da, xp, xi, fd, tp = ({} for k in range(16))
+        at, dyt, x8, ac, g3, g6, g2, dyg, dyq, dyqs, dh, da, xp, xi, tp = ({} for k in range(15))
 
         def load_a(i):
             at[i] = pool.tile([P, 4 * F], BF16, name=f"a{i}", tag="a", bufs=3)
@@ -97,22 +92,13 @@ def tile_lambmlpbackwardstep_t_kernel(tc, x_bytes, x_scale, a, dy, w2, w1, m, v,
                 d[i] = pool.tile([P, 4 * F], F32, name=f"{tag}_{i}", tag=tag, bufs=2)
                 nc.scalar.activation(out=d[i][:], in_=ac[i][:], func=ACT.Gelu, bias=offs[:, k : k + 1])
 
-        def fd_mm(i, h):
-            s = slice(512 * h, 512 * (h + 1))
-            if on_tensor(i, h):
-                fd[i, h] = psum.tile([P, 512], F32, name=f"fd{i}_{h}", tag="fd", bufs=1)
-                nc.tensor.matmul(fd[i, h][:], lhsT=ident_b[:], rhs=g2[i][:, s], start=True, stop=False)
-                nc.tensor.matmul(fd[i, h][:], lhsT=ident[:], rhs=g3[i][:, s], start=False, stop=True)
-
         def fd1(i, h):
             s = slice(512 * h, 512 * (h + 1))
-            if not on_tensor(i, h):
-                nc.vector.scalar_tensor_tensor(out=g3[i][:, s], in0=g2[i][:, s], scalar=-27.0 / 32, in1=g3[i][:, s], op0=MULT, op1=ADD)
+            nc.vector.scalar_tensor_tensor(out=g3[i][:, s], in0=g2[i][:, s], scalar=-27.0 / 32, in1=g3[i][:, s], op0=MULT, op1=ADD)
 
         def fd2(i, h):
             s = slice(512 * h, 512 * (h + 1))
-            part = fd[i, h][:] if on_tensor(i, h) else g3[i][:, s]
-            nc.vector.scalar_tensor_tensor(out=g6[i][:, s], in0=g6[i][:, s], scalar=-5.0 / 32, in1=part, op0=MULT, op1=ADD)
+            nc.vector.scalar_tensor_tensor(out=g6[i][:, s], in0=g6[i][:, s], scalar=-5.0 / 32, in1=g3[i][:, s], op0=MULT, op1=ADD)
 
         def transposes_pe(i, t):
             tp[i, t] = psum.tile([P, NC, 2, P], F32, name=f"tp{i}_{t}", tag="tp", bufs=2)
@@ -224,7 +210,6 @@ def tile_lambmlpbackwardstep_t_kernel(tc, x_bytes, x_scale, a, dy, w2, w1, m, v,
         nc.vector.memset(ones[:], 1.0)
         nc.scalar.activation(out=warm[:, 0:1], in_=warm[:, 1:2], func=ACT.Gelu, bias=offs[:, 0:1])
         make_identity(nc, ident[:])
-        nc.vector.tensor_scalar(out=ident_b[:], in0=ident[:], scalar1=-27.0 / 32, scalar2=None, op0=MULT)
         clamp(0)
 
         def w2_transposes(h):
@@ -264,74 +249,70 @@ def tile_lambmlpbackwardstep_t_kernel(tc, x_bytes, x_scale, a, dy, w2, w1, m, v,
             if s < NG:
                 widen(s, 0)
             if s < NG:
-                transposes_pe(s, 0)
-            if 1 <= s:
-                fd1(s - 1, 0)
-            if s < NG:
-                transposes_pe(s, 1)
-            if s < NG:
                 widen(s, 3)
-            if 1 <= s:
-                q_dy(s - 1)
-            if 1 <= s:
-                fd1(s - 1, 1)
-            if 0 < s < NG:
-                gelu(s, [0])
-            if 2 <= s and s - 2 < NG - 1:
-                q_da(s - 2)
-            if 1 <= s:
-                fd2(s - 1, 0)
-            if 1 <= s:
-                fd_mm(s - 1, 1)
-            if 1 <= s:
-                mm1(s - 1)
-            if 1 <= s:
-                q_x(s - 1, 0)
             if s < NG:
-                copy_t(s, 0)
+                transposes_pe(s, 0)
             if s < NG:
                 transposes_pe(s, 2)
             if s < NG:
                 widen(s, 1)
             if s == 0:
                 prep_w2(w2_banks)
+            if 0 < s < NG:
+                gelu(s, [0])
             if s < NG:
                 widen(s, 2)
+            if 1 <= s:
+                q_dy(s - 1)
             if s < NG:
-                copy_t(s, 1)
+                copy_t(s, 0)
+            if s < NG:
+                copy_t(s, 2)
+            if 1 <= s:
+                fd1(s - 1, 1)
+            if 1 <= s:
+                mm1(s - 1)
+            if 1 <= s:
+                fd1(s - 1, 0)
+            if s < NG:
+                transposes_pe(s, 1)
+            if 1 <= s:
+                fd2(s - 1, 1)
+            if 2 <= s and s - 2 < NG - 1:
+                q_da(s - 2)
+            if 2 <= s and s - 2 < NG - 1:
+                mm2(s - 2, range(LIVE))
+            if 0 < s < NG:
+                gelu(s, [2])
+            if 1 <= s:
+                fd2(s - 1, 0)
+            if 0 < s < NG:
+                gelu(s, [1])
             if s < NG:
                 transposes_pe(s, 3)
             if s + 1 < NG:
                 clamp(s + 1)
-            if 1 <= s:
-                fd2(s - 1, 1)
-            if 0 < s < NG:
-                gelu(s, [1])
             if s < NG:
-                copy_t(s, 2)
+                pair_up(s, 0)
+            if 1 <= s:
+                q_x(s - 1, 0)
+            if s < NG:
+                copy_t(s, 1)
             if s < NG:
                 copy_t(s, 3)
             if 1 <= s:
+                make_da(s - 1)
+            if 1 <= s:
                 q_x(s - 1, 1)
-            if 0 < s < NG:
-                gelu(s, [2])
-            if s < NG:
-                pair_up(s, 0)
-            if s < NG:
-                fd_mm(s, 0)
-            if 2 <= s and s - 2 < NG - 1:
-                mm2(s - 2, range(LIVE))
             if s < NG:
                 pair_up(s, 1)
-            if 1 <= s:
-                make_da(s - 1)
             if s == NG - 1:
                 for b in range(4):
                     w1_norm(b)
                 nc.scalar.activation(out=warm[:, 0:1], in_=warm[:, 1:2], func=ACT.Abs_reciprocal_sqrt)
             if s == NG:
-                for j, tag in ((3, "fd"), (4, "tp"), (5, "tp")):
-                    gbank.append(psum.tile([P, 512], F32, name=f"g{j}", tag=tag, bufs=1 if tag == "fd" else 2))
+                for j, tag in ((4, "tp"), (5, "tp")):
+                    gbank.append(psum.tile([P, 512], F32, name=f"g{j}", tag=tag, bufs=2))
                     for i in range(NG - 1):
                         mm2(i, [j])
         q_da(NG - 1)

@@ -24,11 +24,10 @@ NG = T // 512
 NC = D // 512
 NJ = D // P
 H = 1.5 * 2.0 ** -11
-LIVE = 4
+LIVE = 3
 
 
-def by_plane(i):
-    return i in (1,3,5,7)
+VC = 768
 
 
 def tile_lambmlpbackwardstep_t_kernel(tc, x_bytes, x_scale, a, dy, w2, w1, m, v, out):
@@ -41,6 +40,7 @@ def tile_lambmlpbackwardstep_t_kernel(tc, x_bytes, x_scale, a, dy, w2, w1, m, v,
 
         ident = keep.tile([P, P], F32, name="ident")
         ones = keep.tile([P, P], F32, name="ones")
+        ident_h = keep.tile([P, P], BF16, name="ident_h")
         offs = keep.tile([P, 4], F32, name="offs")
         warm = keep.tile([P, 2], F32, name="warm")
         xs = keep.tile([P, NG, 4], F32, name="xs")
@@ -68,7 +68,7 @@ def tile_lambmlpbackwardstep_t_kernel(tc, x_bytes, x_scale, a, dy, w2, w1, m, v,
         dy_v = dy.rearrange("(g p t) d -> g p t d", p=P, t=4)
         x_v = x_bytes.rearrange("(g p t) d -> g p t d", p=P, t=4)
 
-        at, dyt, x8, ac, g3, g6, g2, dyg, dyq, dyqs, dh, da, xp, xi, tp = ({} for k in range(15))
+        at, dyt, x8, ac, g3, g6, g2, dyg, dyq, dyqs, dh, da, xp, xi, tp, xw, wb = ({} for k in range(17))
 
         def load_a(i):
             at[i] = pool.tile([P, 4 * F], BF16, name=f"a{i}", tag="a", bufs=3)
@@ -92,13 +92,11 @@ def tile_lambmlpbackwardstep_t_kernel(tc, x_bytes, x_scale, a, dy, w2, w1, m, v,
                 d[i] = pool.tile([P, 4 * F], F32, name=f"{tag}_{i}", tag=tag, bufs=2)
                 nc.scalar.activation(out=d[i][:], in_=ac[i][:], func=ACT.Gelu, bias=offs[:, k : k + 1])
 
-        def fd1(i, h):
-            s = slice(512 * h, 512 * (h + 1))
-            nc.vector.scalar_tensor_tensor(out=g3[i][:, s], in0=g2[i][:, s], scalar=-27.0 / 32, in1=g3[i][:, s], op0=MULT, op1=ADD)
+        def fd1(i):
+            nc.vector.scalar_tensor_tensor(out=g3[i][:], in0=g2[i][:], scalar=-27.0 / 32, in1=g3[i][:], op0=MULT, op1=ADD)
 
-        def fd2(i, h):
-            s = slice(512 * h, 512 * (h + 1))
-            nc.vector.scalar_tensor_tensor(out=g6[i][:, s], in0=g6[i][:, s], scalar=-5.0 / 32, in1=g3[i][:, s], op0=MULT, op1=ADD)
+        def fd2(i):
+            nc.vector.scalar_tensor_tensor(out=g6[i][:], in0=g6[i][:], scalar=-5.0 / 32, in1=g3[i][:], op0=MULT, op1=ADD)
 
         def transposes_pe(i, t):
             tp[i, t] = psum.tile([P, NC, 2, P], F32, name=f"tp{i}_{t}", tag="tp", bufs=2)
@@ -124,33 +122,32 @@ def tile_lambmlpbackwardstep_t_kernel(tc, x_bytes, x_scale, a, dy, w2, w1, m, v,
                     in_=dyg[i][:, s].rearrange("p t k -> p (t k)"),
                 )
 
-        def mm1(i):
-            for h in range(2):
-                dh[i, h] = psum.tile([P, 4, P], F32, name=f"dh{i}_{h}", tag="dh", bufs=2)
-                for t in range(4):
-                    for c in range(NC):
-                        nc.tensor.matmul_mx(
-                            out=dh[i, h][:, t, :],
-                            lhsT=dyq[i][:, t, c, :].bitcast(FP8X4),
-                            lhsT_scale=dyqs[i][:, t, c, :],
-                            rhs=w2q[:, c, 128 * h : 128 * (h + 1)].bitcast(FP8X4),
-                            rhs_scale=w2qs[:, c, 128 * h : 128 * (h + 1)],
-                            start=(c == 0),
-                            stop=(c == NC - 1),
-                        )
+        def mm1(i, h):
+            dh[i, h] = psum.tile([P, 4, P], F32, name=f"dh{i}_{h}", tag="dh", bufs=2)
+            for t in range(4):
+                for c in range(NC):
+                    nc.tensor.matmul_mx(
+                        out=dh[i, h][:, t, :],
+                        lhsT=dyq[i][:, t, c, :].bitcast(FP8X4),
+                        lhsT_scale=dyqs[i][:, t, c, :],
+                        rhs=w2q[:, c, P * h : P * (h + 1)].bitcast(FP8X4),
+                        rhs_scale=w2qs[:, c, P * h : P * (h + 1)],
+                        start=(c == 0),
+                        stop=(c == NC - 1),
+                    )
 
-        def make_da(i):
-            da[i] = pool.tile([P, F, 4], BF16, name=f"da{i}", tag="da", bufs=2, align_bytes=64)
-            wv = g6[i][:].rearrange("p (t f) -> p f t", t=4)
-            for h in range(2):
-                nc.vector.scalar_tensor_tensor(
-                    out=da[i][:, 128 * h : 128 * (h + 1), :],
-                    in0=wv[:, 128 * h : 128 * (h + 1), :],
-                    scalar=4.0 / (15.0 * H),
-                    in1=dh[i, h][:].rearrange("p t f -> p f t"),
-                    op0=MULT,
-                    op1=MULT,
-                )
+        def make_da(i, h):
+            if h == 0:
+                da[i] = pool.tile([P, F, 4], BF16, name=f"da{i}", tag="da", bufs=2, align_bytes=64)
+            s = slice(128 * h, 128 * (h + 1))
+            nc.vector.scalar_tensor_tensor(
+                out=da[i][:, s, :],
+                in0=g6[i][:].rearrange("p (t f) -> p f t", t=4)[:, s, :],
+                scalar=4.0 / (15.0 * H),
+                in1=dh[i, h][:].rearrange("p t f -> p f t"),
+                op0=MULT,
+                op1=MULT,
+            )
 
         def q_da(i):
             nc.vector.quantize_mx(
@@ -159,24 +156,45 @@ def tile_lambmlpbackwardstep_t_kernel(tc, x_bytes, x_scale, a, dy, w2, w1, m, v,
 
         def widen(i, t):
             if t == 0:
-                xp[i] = pool.tile([P, 4 * D], BF16, name=f"xp{i}", tag="xp", bufs=2)
-            if by_plane(i):
-                dst = xp[i][:, D * t : D * (t + 1)]
-            else:
-                dst = xp[i][:].rearrange("p (a d e) -> p a d e", a=2, e=2)[:, t // 2, :, t % 2]
-            nc.vector.tensor_scalar(out=dst, in0=x8[i][:, t, :].bitcast(FP8), scalar1=xs[:, i, t : t + 1], scalar2=None, op0=MULT)
+                xp[i] = pool.tile([P, 2, VC, 2], BF16, name=f"xp{i}", tag="xp", bufs=2)
+            nc.vector.tensor_scalar(
+                out=xp[i][:, t // 2, :, t % 2],
+                in0=x8[i][:, t, 0:VC].bitcast(FP8),
+                scalar1=xs[:, i, t : t + 1],
+                scalar2=None,
+                op0=MULT,
+            )
+
+        def widen_s(i, t):
+            if t == 0:
+                xw[i] = pool.tile([P, 4, D - VC], BF16, name=f"xw{i}", tag="xw", bufs=2)
+            nc.scalar.activation(out=xw[i][:, t, :], in_=x8[i][:, t, VC:D].bitcast(FP8), func=ACT.Copy, scale=xs[:, i, t : t + 1])
 
         def pair_up(i, h):
             if h == 0:
                 xi[i] = pool.tile([P, D * 4], BF16, name=f"xi{i}", tag="xi", bufs=2, align_bytes=64)
-            s = slice(512 * h, 512 * (h + 1))
-            if by_plane(i):
-                src = xp[i][:].rearrange("p (t d) -> p d t", t=4)
-                dst = xi[i][:].rearrange("p (d t) -> p d t", t=4)
-            else:
-                src = xp[i][:].bitcast(F32).rearrange("p (a d) -> p d a", a=2)
-                dst = xi[i][:].bitcast(F32).rearrange("p (d a) -> p d a", a=2)
+            src = xp[i][:].rearrange("p a d e -> p (a d e)").bitcast(F32).rearrange("p (a d) -> p d a", a=2)
+            dst = xi[i][:].bitcast(F32).rearrange("p (d a) -> p d a", a=2)
+            s = slice(512 * h, min(512 * (h + 1), VC))
             nc.scalar.copy(out=dst[:, s, :], in_=src[:, s, :])
+
+        def weave(i, c):
+            half = (D - VC) // 2
+            wb[i, c] = psum.tile([P, 4 * half], BF16, name=f"wb{i}_{c}", tag="wb", bufs=1)
+            step = half if half <= 128 else half // 2
+            for d in range(0, half, step):
+                col = half * c + d
+                nc.tensor.matmul(
+                    wb[i, c][:, 4 * d : 4 * (d + step)],
+                    lhsT=ident_h[:],
+                    rhs=xw[i][:, :, col : col + step].rearrange("p t d -> p d t"),
+                    start=True,
+                    stop=True,
+                )
+
+        def plane_up(i, c):
+            half = (D - VC) // 2
+            nc.scalar.copy(out=xi[i][:, 4 * (VC + half * c) : 4 * (VC + half * (c + 1))], in_=wb[i, c][:])
 
         def q_x(i, h):
             s = slice(512 * h, 512 * (h + 1))
@@ -210,6 +228,7 @@ def tile_lambmlpbackwardstep_t_kernel(tc, x_bytes, x_scale, a, dy, w2, w1, m, v,
         nc.vector.memset(ones[:], 1.0)
         nc.scalar.activation(out=warm[:, 0:1], in_=warm[:, 1:2], func=ACT.Gelu, bias=offs[:, 0:1])
         make_identity(nc, ident[:])
+        nc.vector.tensor_copy(out=ident_h[:], in_=ident[:])
         clamp(0)
 
         def w2_transposes(h):
@@ -250,10 +269,36 @@ def tile_lambmlpbackwardstep_t_kernel(tc, x_bytes, x_scale, a, dy, w2, w1, m, v,
                 widen(s, 0)
             if s < NG:
                 widen(s, 3)
+            if 2 <= s and s - 2 < NG - 1:
+                q_da(s - 2)
+            if 1 <= s:
+                fd1(s - 1)
+            if s < NG:
+                widen(s, 2)
+            if s < NG:
+                widen_s(s, 0)
+            if s < NG:
+                widen_s(s, 3)
+            if 0 < s < NG:
+                gelu(s, [1])
+            if s < NG:
+                widen_s(s, 1)
+            if 2 <= s and s - 2 < NG - 1:
+                mm2(s - 2, range(LIVE))
             if s < NG:
                 transposes_pe(s, 0)
+            if 1 <= s:
+                q_dy(s - 1)
+            if 1 <= s:
+                mm1(s - 1, 0)
+            if 1 <= s:
+                mm1(s - 1, 1)
             if s < NG:
-                transposes_pe(s, 2)
+                widen_s(s, 2)
+            if s < NG:
+                weave(s, 0)
+            if s < NG:
+                copy_t(s, 0)
             if s < NG:
                 widen(s, 1)
             if s == 0:
@@ -261,58 +306,48 @@ def tile_lambmlpbackwardstep_t_kernel(tc, x_bytes, x_scale, a, dy, w2, w1, m, v,
             if 0 < s < NG:
                 gelu(s, [0])
             if s < NG:
-                widen(s, 2)
-            if 1 <= s:
-                q_dy(s - 1)
+                transposes_pe(s, 2)
             if s < NG:
-                copy_t(s, 0)
+                pair_up(s, 0)
             if s < NG:
                 copy_t(s, 2)
             if 1 <= s:
-                fd1(s - 1, 1)
-            if 1 <= s:
-                mm1(s - 1)
-            if 1 <= s:
-                fd1(s - 1, 0)
+                fd2(s - 1)
             if s < NG:
                 transposes_pe(s, 1)
-            if 1 <= s:
-                fd2(s - 1, 1)
-            if 2 <= s and s - 2 < NG - 1:
-                q_da(s - 2)
-            if 2 <= s and s - 2 < NG - 1:
-                mm2(s - 2, range(LIVE))
-            if 0 < s < NG:
-                gelu(s, [2])
-            if 1 <= s:
-                fd2(s - 1, 0)
-            if 0 < s < NG:
-                gelu(s, [1])
-            if s < NG:
-                transposes_pe(s, 3)
             if s + 1 < NG:
                 clamp(s + 1)
-            if s < NG:
-                pair_up(s, 0)
-            if 1 <= s:
-                q_x(s - 1, 0)
-            if s < NG:
-                copy_t(s, 1)
-            if s < NG:
-                copy_t(s, 3)
-            if 1 <= s:
-                make_da(s - 1)
             if 1 <= s:
                 q_x(s - 1, 1)
             if s < NG:
+                plane_up(s, 0)
+            if s < NG:
                 pair_up(s, 1)
+            if 1 <= s:
+                make_da(s - 1, 0)
+            if 1 <= s:
+                make_da(s - 1, 1)
+            if s < NG:
+                copy_t(s, 1)
+            if s < NG:
+                transposes_pe(s, 3)
+            if s < NG:
+                copy_t(s, 3)
+            if s < NG:
+                weave(s, 1)
+            if 0 < s < NG:
+                gelu(s, [2])
+            if s < NG:
+                plane_up(s, 1)
+            if 1 <= s:
+                q_x(s - 1, 0)
             if s == NG - 1:
                 for b in range(4):
                     w1_norm(b)
                 nc.scalar.activation(out=warm[:, 0:1], in_=warm[:, 1:2], func=ACT.Abs_reciprocal_sqrt)
             if s == NG:
-                for j, tag in ((4, "tp"), (5, "tp")):
-                    gbank.append(psum.tile([P, 512], F32, name=f"g{j}", tag=tag, bufs=2))
+                for j, tag in ((3, "wb"), (4, "tp"), (5, "tp")):
+                    gbank.append(psum.tile([P, 512], F32, name=f"g{j}", tag=tag, bufs=1 if tag == "wb" else 2))
                     for i in range(NG - 1):
                         mm2(i, [j])
         q_da(NG - 1)
@@ -350,6 +385,9 @@ def tile_lambmlpbackwardstep_t_kernel(tc, x_bytes, x_scale, a, dy, w2, w1, m, v,
 
         moments(0)
         moments(1)
+        tot = psum.tile([P, 8], F32, name="tot", tag="g0", bufs=1)
+        for b in range(4):
+            nc.tensor.matmul(tot[:, 1:2], lhsT=ones[:], rhs=stats[:, b : b + 1], start=(b == 0), stop=(b == 3))
         moments(2)
         inv_root(0)
         moments(3)
@@ -361,16 +399,13 @@ def tile_lambmlpbackwardstep_t_kernel(tc, x_bytes, x_scale, a, dy, w2, w1, m, v,
         r_norm(0)
         inv_root(3)
         ratio(2)
+        nc.vector.reciprocal(out=wsum[:, 0:1], in_=tot[:, 1:2])
         decay(1)
         r_norm(1)
         ratio(3)
         decay(2)
         r_norm(2)
-        tot = psum.tile([P, 8], F32, name="tot", tag="g0", bufs=1)
-        for b in range(4):
-            nc.tensor.matmul(tot[:, 1:2], lhsT=ones[:], rhs=stats[:, b : b + 1], start=(b == 0), stop=(b == 3))
         decay(3)
-        nc.vector.reciprocal(out=wsum[:, 0:1], in_=tot[:, 1:2])
         r_norm(3)
         for b in range(4):
             nc.tensor.matmul(tot[:, 0:1], lhsT=ones[:], rhs=stats[:, 4 + b : 5 + b], start=(b == 0), stop=(b == 3))

from contextlib import ExitStack

import concourse.mybir as mybir
from concourse.masks import make_identity

F32 = mybir.dt.float32
BF16 = mybir.dt.bfloat16
U32 = mybir.dt.uint32
U8 = mybir.dt.uint8
FP8 = mybir.dt.float8_e4m3fn
FP8X4 = mybir.dt.float8_e4m3fn_x4
MULT = mybir.AluOpType.mult
ADD = mybir.AluOpType.add
SUB = mybir.AluOpType.subtract
MAX = mybir.AluOpType.max
MIN = mybir.AluOpType.min
ACT = mybir.ActivationFunctionType

T, D, F = 4096, 1024, 256
FLOPS = 4 * T * D * F

P = 128
NG = T // 512
NC = D // 512
NJ = D // P
H = 1.5 * 2.0 ** -11
LIVE = 3


VC = 768


def tile_lambmlpbackwardstep_t_kernel(tc, x_bytes, x_scale, a, dy, w2, w1, m, v, out):
    nc = tc.nc
    with ExitStack() as ctx:
        keep = ctx.enter_context(tc.tile_pool(name="keep", bufs=1))
        pool = ctx.enter_context(tc.tile_pool(name="work", bufs=2))
        psum = ctx.enter_context(tc.psum_pool(name="psum", bufs=1))
        ctx.enter_context(tc.manual_schedule())

        ident = keep.tile([P, P], F32, name="ident")
        ones = keep.tile([P, P], F32, name="ones")
        ident_h = keep.tile([P, P], BF16, name="ident_h")
        offs = keep.tile([P, 4], F32, name="offs")
        warm = keep.tile([P, 2], F32, name="warm")
        xs = keep.tile([P, NG, 4], F32, name="xs")
        xq = keep.tile([P, NG, D], U32, name="xq", align_bytes=64)
        xqs = keep.tile([P, NG, D], U8, name="xqs", align_bytes=64)
        daq = keep.tile([P, NG, F], U32, name="daq", align_bytes=64)
        daqs = keep.tile([P, NG, F], U8, name="daqs", align_bytes=64)
        w2r = keep.tile([P, 2, D], BF16, name="w2r", align_bytes=64)
        w2g = keep.tile([P, NC * F * 4], BF16, name="w2g", align_bytes=64)
        w2q = keep.tile([P, NC, F], U32, name="w2q", align_bytes=64)
        w2qs = keep.tile([P, NC, F], U8, name="w2qs", align_bytes=64)
        w1t = keep.tile([P, NJ, F], BF16, name="w1t")
        mt = keep.tile([P, NJ, F], BF16, name="mt")
        vt = keep.tile([P, NJ, F], BF16, name="vt")
        sq = keep.tile([P, NJ, F], F32, name="sq")
        mn = keep.tile([P, NJ, F], F32, name="mn")
        stats = keep.tile([P, 8], F32, name="stats")
        small = keep.tile([P, 8], F32, name="small")
        wsum = keep.tile([P, 8], F32, name="wsum")
        junk = keep.tile([P, 2, F], BF16, name="junk")

        gbank = [psum.tile([P, 512], F32, name=f"g{j}", tag=f"g{j}", bufs=1) for j in range(LIVE)]

        a_v = a.rearrange("(g p t) f -> g p t f", p=P, t=4)
        dy_v = dy.rearrange("(g p t) d -> g p t d", p=P, t=4)
        x_v = x_bytes.rearrange("(g p t) d -> g p t d", p=P, t=4)

        at, dyt, x8, ac, g3, g6, g2, dyg, dyq, dyqs, dh, da, xp, xi, tp, xw, wb = ({} for k in range(17))

        def load_a(i):
            at[i] = pool.tile([P, 4 * F], BF16, name=f"a{i}", tag="a", bufs=3)
            nc.sync.dma_start(out=at[i][:].rearrange("p (t f) -> p t f", t=4), in_=a_v[i])

        def load_dy(i):
            dyt[i] = pool.tile([P, 4, D], BF16, name=f"dy{i}", tag="dy", bufs=3)
            nc.sync.dma_start(out=dyt[i][:], in_=dy_v[i])

        def load_x(i):
            x8[i] = pool.tile([P, 4, D], U8, name=f"x8_{i}", tag="x8", bufs=3)
            nc.sync.dma_start(out=x8[i][:], in_=x_v[i])

        def clamp(i):
            ac[i] = pool.tile([P, 4 * F], BF16, name=f"ac{i}", tag="ac", bufs=2)
            nc.vector.tensor_scalar(out=ac[i][:], in0=at[i][:], scalar1=7.0, scalar2=-7.0, op0=MIN, op1=MAX)

        def gelu(i, nodes):
            for n in nodes:
                d, tag, k = ((g2, "g2", 0), (g3, "g3", 1), (g6, "g6", 2))[n]
                d[i] = pool.tile([P, 4 * F], F32, name=f"{tag}_{i}", tag=tag, bufs=2)
                nc.scalar.activation(out=d[i][:], in_=ac[i][:], func=ACT.Gelu, bias=offs[:, k : k + 1])

        def fd1(i):
            nc.vector.scalar_tensor_tensor(out=g3[i][:], in0=g2[i][:], scalar=-27.0 / 32, in1=g3[i][:], op0=MULT, op1=ADD)

        def fd2(i):
            nc.vector.scalar_tensor_tensor(out=g6[i][:], in0=g6[i][:], scalar=-5.0 / 32, in1=g3[i][:], op0=MULT, op1=ADD)

        def transposes_pe(i, t):
            tp[i, t] = psum.tile([P, NC, 2, P], F32, name=f"tp{i}_{t}", tag="tp", bufs=2)
            words = dyt[i][:, t, :].bitcast(F32)
            for c in range(NC):
                for u in range(2):
                    nc.tensor.transpose(tp[i, t][:, c, u, :], words[:, 256 * c + u : 256 * (c + 1) : 2], ident[:])

        def copy_t(i, t):
            if t == 0:
                dyg[i] = pool.tile([P, 4, D], BF16, name=f"dyg{i}", tag="dyg", bufs=2, align_bytes=64)
            dst = dyg[i][:, t, :].bitcast(F32).rearrange("q (c r u) -> q c r u", c=NC, u=2)
            nc.scalar.copy(out=dst, in_=tp[i, t][:].rearrange("q c u r -> q c r u"))

        def q_dy(i):
            dyq[i] = pool.tile([P, 4, NC, P], U32, name=f"dyq{i}", tag="dyq", bufs=2, align_bytes=64)
            dyqs[i] = pool.tile([P, 4, NC, P], U8, name=f"dyqs{i}", tag="dyqs", bufs=2, align_bytes=64)
            for h in range(2):
                s = slice(2 * h, 2 * h + 2)
                nc.vector.quantize_mx(
                    out=dyq[i][:, s].rearrange("p t c r -> p (t c r)").bitcast(FP8X4),
                    scales=dyqs[i][:, s].rearrange("p t c r -> p (t c r)"),
                    in_=dyg[i][:, s].rearrange("p t k -> p (t k)"),
                )

        def mm1(i, h):
            dh[i, h] = psum.tile([P, 4, P], F32, name=f"dh{i}_{h}", tag="dh", bufs=2)
            for t in range(4):
                for c in range(NC):
                    nc.tensor.matmul_mx(
                        out=dh[i, h][:, t, :],
                        lhsT=dyq[i][:, t, c, :].bitcast(FP8X4),
                        lhsT_scale=dyqs[i][:, t, c, :],
                        rhs=w2q[:, c, P * h : P * (h + 1)].bitcast(FP8X4),
                        rhs_scale=w2qs[:, c, P * h : P * (h + 1)],
                        start=(c == 0),
                        stop=(c == NC - 1),
                    )

        def make_da(i, h):
            if h == 0:
                da[i] = pool.tile([P, F, 4], BF16, name=f"da{i}", tag="da", bufs=2, align_bytes=64)
            s = slice(128 * h, 128 * (h + 1))
            nc.vector.scalar_tensor_tensor(
                out=da[i][:, s, :],
                in0=g6[i][:].rearrange("p (t f) -> p f t", t=4)[:, s, :],
                scalar=4.0 / (15.0 * H),
                in1=dh[i, h][:].rearrange("p t f -> p f t"),
                op0=MULT,
                op1=MULT,
            )

        def q_da(i):
            nc.vector.quantize_mx(
                out=daq[:, i, :].bitcast(FP8X4), scales=daqs[:, i, :], in_=da[i][:].rearrange("p f t -> p (f t)")
            )

        def widen(i, t):
            if t == 0:
                xp[i] = pool.tile([P, 2, VC, 2], BF16, name=f"xp{i}", tag="xp", bufs=2)
            nc.vector.tensor_scalar(
                out=xp[i][:, t // 2, :, t % 2],
                in0=x8[i][:, t, 0:VC].bitcast(FP8),
                scalar1=xs[:, i, t : t + 1],
                scalar2=None,
                op0=MULT,
            )

        def widen_s(i, t):
            if t == 0:
                xw[i] = pool.tile([P, 4, D - VC], BF16, name=f"xw{i}", tag="xw", bufs=2)
            nc.scalar.activation(out=xw[i][:, t, :], in_=x8[i][:, t, VC:D].bitcast(FP8), func=ACT.Copy, scale=xs[:, i, t : t + 1])

        def pair_up(i, h):
            if h == 0:
                xi[i] = pool.tile([P, D * 4], BF16, name=f"xi{i}", tag="xi", bufs=2, align_bytes=64)
            src = xp[i][:].rearrange("p a d e -> p (a d e)").bitcast(F32).rearrange("p (a d) -> p d a", a=2)
            dst = xi[i][:].bitcast(F32).rearrange("p (d a) -> p d a", a=2)
            s = slice(512 * h, min(512 * (h + 1), VC))
            nc.scalar.copy(out=dst[:, s, :], in_=src[:, s, :])

        def weave(i, c):
            half = (D - VC) // 2
            wb[i, c] = psum.tile([P, 4 * half], BF16, name=f"wb{i}_{c}", tag="wb", bufs=1)
            step = half if half <= 128 else half // 2
            for d in range(0, half, step):
                col = half * c + d
                nc.tensor.matmul(
                    wb[i, c][:, 4 * d : 4 * (d + step)],
                    lhsT=ident_h[:],
                    rhs=xw[i][:, :, col : col + step].rearrange("p t d -> p d t"),
                    start=True,
                    stop=True,
                )

        def plane_up(i, c):
            half = (D - VC) // 2
            nc.scalar.copy(out=xi[i][:, 4 * (VC + half * c) : 4 * (VC + half * (c + 1))], in_=wb[i, c][:])

        def q_x(i, h):
            s = slice(512 * h, 512 * (h + 1))
            nc.vector.quantize_mx(
                out=xq[:, i, s].bitcast(FP8X4), scales=xqs[:, i, s], in_=xi[i][:, 2048 * h : 2048 * (h + 1)]
            )

        def mm2(i, js):
            for j in js:
                nc.tensor.matmul_mx(
                    out=gbank[j][:, 0:F],
                    lhsT=xq[:, i, P * j : P * (j + 1)].bitcast(FP8X4),
                    lhsT_scale=xqs[:, i, P * j : P * (j + 1)],
                    rhs=daq[:, i, :].bitcast(FP8X4),
                    rhs_scale=daqs[:, i, :],
                    start=(i == 0),
                    stop=(i == NG - 1),
                )

        load_a(0)
        nc.scalar.dma_start(out=xs[:], in_=x_scale.rearrange("(g p t) o -> p g (t o)", p=P, t=4))
        load_x(0)
        nc.sync.dma_start(out=w2r[:], in_=w2.rearrange("(h p) d -> p h d", p=P))
        load_dy(0)
        load_a(1)
        load_x(1)
        load_dy(1)
        nc.vector.memset(warm[:], 1.0)
        for k, n in enumerate((-2.0, 3.0, 6.0)):
            nc.vector.memset(offs[:, k : k + 1], n * H)
        nc.vector.memset(ones[:], 1.0)
        nc.scalar.activation(out=warm[:, 0:1], in_=warm[:, 1:2], func=ACT.Gelu, bias=offs[:, 0:1])
        make_identity(nc, ident[:])
        nc.vector.tensor_copy(out=ident_h[:], in_=ident[:])
        clamp(0)

        def w2_transposes(h):
            bank = psum.tile([P, NC, 2, P], F32, name=f"w2_{h}", tag="dh", bufs=2)
            words = w2r[:, h, :].bitcast(F32)
            for c in range(NC):
                for u in range(2):
                    nc.tensor.transpose(bank[:, c, u, :], words[:, 256 * c + u : 256 * (c + 1) : 2], ident[:])
            return bank

        def prep_w2(banks):
            dst = w2g[:].bitcast(F32).rearrange("q (c f u) -> q c f u", c=NC, u=2)
            for h in range(2):
                nc.vector.tensor_copy(out=dst[:, :, P * h : P * (h + 1), :], in_=banks[h][:].rearrange("q c u r -> q c r u"))
            nc.vector.quantize_mx(
                out=w2q[:].rearrange("p c f -> p (c f)").bitcast(FP8X4), scales=w2qs[:].rearrange("p c f -> p (c f)"), in_=w2g[:]
            )

        def w1_norm(b):
            s = slice(2 * b, 2 * b + 2)
            nc.scalar.activation(out=junk[:], in_=w1t[:, s, :], func=ACT.Square, scale=0.5, accum_out=stats[:, b : b + 1])

        for s in range(NG + 1):
            if s + 2 < NG:
                load_a(s + 2)
                load_x(s + 2)
                load_dy(s + 2)
            if s == 2:
                nc.sync.dma_start(out=w1t[:], in_=w1.rearrange("(j p) f -> p j f", p=P))
            if s == 4:
                nc.sync.dma_start(out=mt[:], in_=m.rearrange("(j p) f -> p j f", p=P))
                nc.sync.dma_start(out=vt[:], in_=v.rearrange("(j p) f -> p j f", p=P))
            if s == 0:
                w2_banks = [w2_transposes(h) for h in range(2)]
            if s == 0:
                gelu(0, range(3))
            if s < NG:
                widen(s, 0)
            if s < NG:
                widen(s, 3)
            if 2 <= s and s - 2 < NG - 1:
                q_da(s - 2)
            if 1 <= s:
                fd1(s - 1)
            if s < NG:
                widen(s, 2)
            if s < NG:
                widen_s(s, 0)
            if s < NG:
                widen_s(s, 3)
            if 0 < s < NG:
                gelu(s, [1])
            if s < NG:
                widen_s(s, 1)
            if 2 <= s and s - 2 < NG - 1:
                mm2(s - 2, range(LIVE))
            if s < NG:
                transposes_pe(s, 0)
            if 1 <= s:
                q_dy(s - 1)
            if 1 <= s:
                mm1(s - 1, 0)
            if 1 <= s:
                mm1(s - 1, 1)
            if s < NG:
                widen_s(s, 2)
            if s < NG:
                weave(s, 0)
            if s < NG:
                copy_t(s, 0)
            if s < NG:
                widen(s, 1)
            if s == 0:
                prep_w2(w2_banks)
            if 0 < s < NG:
                gelu(s, [0])
            if s < NG:
                transposes_pe(s, 2)
            if s < NG:
                pair_up(s, 0)
            if s < NG:
                copy_t(s, 2)
            if 1 <= s:
                fd2(s - 1)
            if s < NG:
                transposes_pe(s, 1)
            if s + 1 < NG:
                clamp(s + 1)
            if 1 <= s:
                q_x(s - 1, 1)
            if s < NG:
                plane_up(s, 0)
            if s < NG:
                pair_up(s, 1)
            if 1 <= s:
                make_da(s - 1, 0)
            if 1 <= s:
                make_da(s - 1, 1)
            if s < NG:
                copy_t(s, 1)
            if s < NG:
                transposes_pe(s, 3)
            if s < NG:
                copy_t(s, 3)
            if s < NG:
                weave(s, 1)
            if 0 < s < NG:
                gelu(s, [2])
            if s < NG:
                plane_up(s, 1)
            if 1 <= s:
                q_x(s - 1, 0)
            if s == NG - 1:
                for b in range(4):
                    w1_norm(b)
                nc.scalar.activation(out=warm[:, 0:1], in_=warm[:, 1:2], func=ACT.Abs_reciprocal_sqrt)
            if s == NG:
                for j, tag in ((3, "wb"), (4, "tp"), (5, "tp")):
                    gbank.append(psum.tile([P, 512], F32, name=f"g{j}", tag=tag, bufs=1 if tag == "wb" else 2))
                    for i in range(NG - 1):
                        mm2(i, [j])
        q_da(NG - 1)
        mm2(NG - 1, range(6))
        for j in (6, 7):
            gbank.append(psum.tile([P, 512], F32, name=f"g{j}", tag="dh", bufs=2))
            for i in range(NG):
                mm2(i, [j])
        def moments(b):
            for js, jv in ((2 * b, 2 * b + 1), (2 * b + 1, 2 * b)):
                nc.scalar.activation(
                    out=sq[:, js, :], in_=gbank[js][:, 0:F], func=ACT.Square, scale=(2.0 / 3.0) ** 0.5 / 64.0
                )
                nc.vector.scalar_tensor_tensor(
                    out=mn[:, jv, :], in0=gbank[jv][:, 0:F], scalar=-2.0 / 3.0 / 64.0, in1=mt[:, jv, :], op0=MULT, op1=SUB
                )
            s = slice(2 * b, 2 * b + 2)
            nc.gpsimd.tensor_tensor(out=sq[:, s, :], in0=sq[:, s, :], in1=vt[:, s, :], op=ADD)

        def inv_root(b):
            s = slice(2 * b, 2 * b + 2)
            nc.scalar.activation(out=sq[:, s, :], in_=sq[:, s, :], func=ACT.Abs_reciprocal_sqrt, scale=1.0 / 0.6)

        def ratio(b):
            s = slice(2 * b, 2 * b + 2)
            nc.vector.tensor_tensor(out=mn[:, s, :], in0=mn[:, s, :], in1=sq[:, s, :], op=MULT)

        def decay(b):
            s = slice(2 * b, 2 * b + 2)
            nc.vector.scalar_tensor_tensor(out=mn[:, s, :], in0=w1t[:, s, :], scalar=-0.1, in1=mn[:, s, :], op0=MULT, op1=ADD)

        def r_norm(b):
            s = slice(2 * b, 2 * b + 2)
            nc.scalar.activation(out=sq[:, s, :], in_=mn[:, s, :], func=ACT.Square, accum_out=stats[:, 4 + b : 5 + b])

        moments(0)
        moments(1)
        tot = psum.tile([P, 8], F32, name="tot", tag="g0", bufs=1)
        for b in range(4):
            nc.tensor.matmul(tot[:, 1:2], lhsT=ones[:], rhs=stats[:, b : b + 1], start=(b == 0), stop=(b == 3))
        moments(2)
        inv_root(0)
        moments(3)
        inv_root(1)
        ratio(0)
        inv_root(2)
        ratio(1)
        decay(0)
        r_norm(0)
        inv_root(3)
        ratio(2)
        nc.vector.reciprocal(out=wsum[:, 0:1], in_=tot[:, 1:2])
        decay(1)
        r_norm(1)
        ratio(3)
        decay(2)
        r_norm(2)
        decay(3)
        r_norm(3)
        for b in range(4):
            nc.tensor.matmul(tot[:, 0:1], lhsT=ones[:], rhs=stats[:, 4 + b : 5 + b], start=(b == 0), stop=(b == 3))
        nc.scalar.activation(out=small[:, 0:1], in_=tot[:, 0:1], func=ACT.Abs_reciprocal_sqrt, scale=wsum[:, 0:1])
        out_v = out.rearrange("(j p) f -> p j f", p=P)
        for b in range(4):
            s = slice(2 * b, 2 * b + 2)
            res = pool.tile([P, 2, F], F32, name=f"res{b}", tag="res", bufs=4)
            nc.vector.scalar_tensor_tensor(
                out=res[:], in0=mn[:, s, :], scalar=small[:, 0:1], in1=w1t[:, s, :], op0=MULT, op1=ADD
            )
            nc.sync.dma_start(out=out_v[:, s, :], in_=res[:])
